import numpy as np
import ml_dtypes


def mxq(x, axis, fmt="e4m3"):
    dtype, down = {"e4m3": (ml_dtypes.float8_e4m3fn, 7), "e5m2": (ml_dtypes.float8_e5m2, 14)}[fmt]
    v = np.moveaxis(np.asarray(x, np.float32).astype(ml_dtypes.bfloat16).astype(np.float64), axis, -1)
    blocks = v.reshape(v.shape[:-1] + (-1, 32))
    amax = np.abs(blocks).max(-1, keepdims=True)
    byte = np.maximum(np.where(amax > 0, np.frexp(amax)[1] - 1 + 127, 0) - down, 1)
    scale = np.exp2(byte - 127.0)
    codes = (blocks / scale).astype(np.float32).astype(dtype).astype(np.float64)
    return np.moveaxis((codes * scale).reshape(v.shape), -1, axis)


WIDE = False


def mx_kscale(k):
    if not WIDE:
        return np.ones(k)
    levels = np.array([10, -10, 5, -5, 0])
    if k % 512:
        return np.exp2(np.random.permutation(np.resize(levels, k // 32))).repeat(32)
    a = np.empty((k // 512, 16))
    for p in range(k // 512):
        a[p, :8] = np.random.permutation(np.resize(levels, 8))
        for g in range(8):
            far = levels[np.abs(levels - a[p, g]) >= 10]
            a[p, g + 8] = far[np.random.randint(len(far))]
    return np.exp2(a.ravel()).repeat(32)


def f64(x):
    return np.asarray(x).astype(np.float64)


def striped(idx):
    return np.tile(idx.reshape(-1, 16).T, (8, 1)).astype(np.uint16)


def unstriped(offs):
    return offs[:16].T.reshape(-1).astype(np.int64)


def d_relu2(v):
    return 2.0 * np.maximum(v, 0.0)


K, T, E, C, H, N = 256, 2048, 4, 256, 1024, 512


def by_expert(wq, xq):
    return np.concatenate([wq[e].T @ xq[:, e * C:(e + 1) * C] for e in range(E)], axis=1)


def setup_inputs():
    n = np.random.standard_normal
    s = mx_kscale(N)[:, None]
    u = mx_kscale(H)
    return {
        "dyT": (n((N, T)) * s).astype(np.float32),
        "a": n((H, E * C)).astype(np.float32),
        "w2": (n((E, N, H)) / np.sqrt(N) / s[None] * u[None, None, :]).astype(np.float32),
        "w1": (n((E, H, K)) / np.sqrt(H) / u[None, :, None]).astype(np.float32),
        "gate": np.tile(np.random.uniform(0.2, 1.0, E * C), (N, 1)).astype(np.float32),
        "offs": striped(np.random.permutation(T)[:E * C]),
    }


def reference(dyT, a, w2, w1, gate, offs):
    idx = unstriped(offs)
    gq = mxq(f64(gate) * f64(dyT)[:, idx], 0, "e4m3")
    dh = by_expert(mxq(f64(w2), 1, "e4m3"), gq)
    da = dh * d_relu2(f64(a))
    dx = by_expert(mxq(f64(w1), 1, "e4m3"), mxq(da, 0, "e4m3"))
    out = np.zeros((K, T))
    out[:, idx] = dx
    return out

@@ -1,0 +1,273 @@
+from contextlib import ExitStack
+
+import concourse.mybir as mybir
+from concourse.masks import make_identity
+
+K, T, E, C, H, N = 256, 2048, 4, 256, 1024, 512
+S = E * C
+
+FLOPS = 2 * S * H * (N + K)
+BYTES = 4 * (N * T + H * S + E * N * H + E * H * K + S + K * T) + 2 * 128 * (S // 16)
+
+F32 = mybir.dt.float32
+BF16 = mybir.dt.bfloat16
+U32 = mybir.dt.uint32
+U16 = mybir.dt.uint16
+U8 = mybir.dt.uint8
+FP8X4 = mybir.dt.float8_e4m3fn_x4
+
+ALU = mybir.AluOpType
+COPY = mybir.ActivationFunctionType.Copy
+
+P = 128
+PACK = 4
+Q = H // (P * PACK)
+R = K // P
+HALF = 128
+PIECES = ((0, 128), (128, 512), (512, 1024))
+
+
+def tile_moe_bdx_mlp_relu2_kernel(tc, dyT, a, w2, w1, gate, offs, out):
+    nc = tc.nc
+    dy_rows = dyT.rearrange("(p j) t -> p j t", j=PACK)
+    a_rows = a.rearrange("(q p t) s -> q p t s", q=Q, t=PACK)
+    w2_rows = w2.rearrange("e (p j) i -> e p j i", j=PACK)
+    w1_rows = w1.rearrange("e (q p t) k -> e p q t k", q=Q, t=PACK)
+
+    with ExitStack() as ctx:
+        held = ctx.enter_context(tc.tile_pool(name="held", bufs=1))
+        raw = ctx.enter_context(tc.tile_pool(name="raw", bufs=11))
+        work = ctx.enter_context(tc.tile_pool(name="work", bufs=2))
+        psum = ctx.enter_context(tc.psum_pool(name="psum", bufs=1))
+
+        offsets = held.tile([P, S // 16], U16, name="offsets")
+        gates = held.tile([P, S], F32, name="gates")
+        nc.sync.dma_start(gates[:, 0:P], gate[0:P, 0:P])
+        nc.sync.dma_start(offsets[:], offs)
+        gate_rows = held.tile([P, P], F32, name="gate_rows")
+        nc.scalar.dma_start(gate_rows[:], gate[0 : P * P // S, :].rearrange("r (b c) -> (r b) c", c=P))
+        identity = held.tile([P, P], F32, name="identity")
+        make_identity(nc, identity[:])
+
+        windows = []
+        for r in range(R):
+            window = held.tile([P, T], F32, name=f"window{r}")
+            nc.gpsimd.memset(window[:], 0.0)
+            windows.append(window)
+
+        def load(view, name, shape, tag="raw", bufs=None):
+            t = raw.tile(shape, F32, name=name, tag=tag) if bufs is None else raw.tile(shape, F32, name=name, tag=tag, bufs=bufs)
+            nc.sync.dma_start(t[:], view)
+            return t
+
+        dy, w2_raw, w1_raw, a_raw = {}, {}, {}, {}
+
+        def load_dy(j):
+            dy[j] = load(dy_rows[:, j, :], f"dy{j}", [P, T])
+
+        def load_w2(e, halves=False):
+            w2_raw[e] = raw.tile([P, PACK, H], F32, name=f"w2raw{e}", tag="w2raw", bufs=3)
+            step = 512 if halves else H
+            for c in range(0, H, step):
+                nc.sync.dma_start(w2_raw[e][:, :, c : c + step], w2_rows[e, :, :, c : c + step])
+
+        def load_w1(e, halves=False):
+            w1_raw[e] = raw.tile([P, Q, PACK, K], F32, name=f"w1raw{e}", tag="raw")
+            if halves:
+                for q in range(Q):
+                    nc.sync.dma_start(w1_raw[e][:, q], w1_rows[e, :, q])
+            else:
+                nc.sync.dma_start(w1_raw[e][:], w1_rows[e])
+
+        def load_a(h, q):
+            a_raw[h, q] = load(a_rows[q, :, :, h * 512 : (h + 1) * 512], f"araw{h}{q}", [P, PACK, 512])
+
+        load_dy(0)
+        for j in range(1, PACK):
+            load_dy(j)
+        load_w2(0)
+        load_w2(1)
+        load_a(0, 0)
+        load_a(0, 1)
+        load_w1(0)
+        load_w1(1)
+        load_w2(2)
+        load_w2(3)
+        load_a(1, 0)
+        load_a(1, 1)
+        load_w1(2)
+        load_w1(3, halves=True)
+
+        turned = psum.tile([P, P], F32, name="turned", tag="dx", bufs=2)
+        nc.tensor.transpose(turned[:], gate_rows[:], identity[:])
+        gate_cols = held.tile([P, S // P], F32, name="gate_cols")
+        nc.scalar.copy(gate_cols[:], turned[:, 0 : S // P])
+        for s0, s1 in PIECES[1:]:
+            spread = psum.tile([P, 512], F32, name="spread", tag="dx", bufs=2)
+            for c in range(s0, s1, P):
+                nc.tensor.transpose(
+                    spread[:, c - s0 : c - s0 + P], gate_cols[:, c // P : c // P + 1].to_broadcast([P, P]), identity[:]
+                )
+            nc.scalar.copy(gates[:, s0:s1], spread[:, 0 : s1 - s0])
+
+        g4 = held.tile([P, PACK, S], F32, name="g4")
+        g_codes = held.tile([P, S], U32, name="g_codes", align_bytes=64)
+        g_scales = held.tile([P, S], U8, name="g_scales", align_bytes=64)
+        w2_codes, w2_scales, w1_codes, w1_scales, da, dxs, vb = {}, {}, {}, {}, {}, {}, {}
+
+        def gather(j, s0, s1):
+            nc.vector.tensor_tensor(
+                g4[:, j, s0:s1], dy[j][:].indirect(offsets[:, s0 // 16 : s1 // 16]), gates[:, s0:s1], ALU.mult
+            )
+
+        def quantise_g(e, copy):
+            gb = work.tile([P, PACK * C], BF16, name="gb", align_bytes=64)
+            cols = slice(e * C, (e + 1) * C)
+            copy(
+                out=gb[:].rearrange("p (c i j) -> p c j i", i=4, j=PACK),
+                in_=g4[:, :, cols].rearrange("p j (c i) -> p c j i", i=4),
+            )
+            nc.vector.quantize_mx(out=g_codes[:, cols].bitcast(FP8X4), scales=g_scales[:, cols], in_=gb[:])
+
+        def quantise_w2(e, copies):
+            w2_codes[e] = work.tile([P, H], U32, name="w2_codes", align_bytes=64)
+            w2_scales[e] = work.tile([P, H], U8, name="w2_scales", align_bytes=64)
+            for q in range(Q):
+                cols = slice(q * 512, (q + 1) * 512)
+                wb = work.tile([P, PACK * 512], BF16, name="wb", align_bytes=64, bufs=3)
+                copies[q](
+                    out=wb[:].rearrange("p (t m j) -> p m j t", t=PACK, j=PACK),
+                    in_=w2_raw[e][:, :, cols].rearrange("p j (m t) -> p m j t", t=PACK),
+                )
+                nc.vector.quantize_mx(out=w2_codes[e][:, cols].bitcast(FP8X4), scales=w2_scales[e][:, cols], in_=wb[:])
+
+        def start_w1(e):
+            w1_codes[e] = work.tile([P, Q, K], U32, name="w1_codes", align_bytes=64)
+            w1_scales[e] = work.tile([P, Q, K], U8, name="w1_scales", align_bytes=64)
+            vb[e] = work.tile([P, Q, K * PACK], BF16, name="vb", align_bytes=64)
+
+        def round_w1(e, q, c0, c1, copy):
+            copy(
+                out=vb[e][:, q, c0 * PACK : c1 * PACK].rearrange("p (c i t) -> p c t i", i=4, t=PACK),
+                in_=w1_raw[e][:, q, :, c0:c1].rearrange("p t (c i) -> p c t i", i=4),
+            )
+
+        def quantise_w1(e):
+            nc.vector.quantize_mx(
+                out=w1_codes[e][:].rearrange("p q k -> p (q k)").bitcast(FP8X4),
+                scales=w1_scales[e][:].rearrange("p q k -> p (q k)"),
+                in_=vb[e][:].rearrange("p q k -> p (q k)"),
+            )
+
+        def quantise_w1_part(e, q, c0, c1):
+            nc.vector.quantize_mx(
+                out=w1_codes[e][:, q, c0:c1].bitcast(FP8X4),
+                scales=w1_scales[e][:, q, c0:c1],
+                in_=vb[e][:, q, c0 * PACK : c1 * PACK],
+            )
+
+        def hidden(e):
+            db = {}
+            for q in range(Q):
+                db[q] = work.tile([P, C, PACK], BF16, name="db", align_bytes=64, bufs=3)
+                for h in range(C // HALF):
+                    dh = psum.tile([P, PACK, HALF], F32, name="dh", bufs=6)
+                    s0 = e * C + h * HALF
+                    for t in range(PACK):
+                        wc = slice(q * 512 + t * P, q * 512 + (t + 1) * P)
+                        nc.tensor.matmul_mx(
+                            out=dh[:, t, :],
+                            lhsT=w2_codes[e][:, wc].bitcast(FP8X4),
+                            lhsT_scale=w2_scales[e][:, wc],
+                            rhs=g_codes[:, s0 : s0 + HALF].bitcast(FP8X4),
+                            rhs_scale=g_scales[:, s0 : s0 + HALF],
+                            start=True,
+                            stop=True,
+                        )
+                    ac = (e % 2) * C + h * HALF
+                    nc.vector.scalar_tensor_tensor(
+                        out=db[q][:, h * HALF : (h + 1) * HALF, :],
+                        in0=a_raw[e // 2, q][:, :, ac : ac + HALF].rearrange("p t s -> p s t"),
+                        scalar=0.0,
+                        in1=dh[:].rearrange("p t s -> p s t"),
+                        op0=ALU.max,
+                        op1=ALU.mult,
+                    )
+            codes = work.tile([P, Q, C], U32, name="da_codes", align_bytes=64)
+            scales = work.tile([P, Q, C], U8, name="da_scales", align_bytes=64)
+            for q in range(Q):
+                nc.vector.quantize_mx(
+                    out=codes[:, q, :].bitcast(FP8X4),
+                    scales=scales[:, q, :],
+                    in_=db[q][:].rearrange("p s t -> p (s t)"),
+                )
+            da[e] = (codes, scales)
+
+        def back(e, r):
+            codes, scales = da[e]
+            dx = psum.tile([P, C], F32, name="dx", tag="dx", bufs=2)
+            for q in range(Q):
+                nc.tensor.matmul_mx(
+                    out=dx[:],
+                    lhsT=w1_codes[e][:, q, r * P : (r + 1) * P].bitcast(FP8X4),
+                    lhsT_scale=w1_scales[e][:, q, r * P : (r + 1) * P],
+                    rhs=codes[:, q, :].bitcast(FP8X4),
+                    rhs_scale=scales[:, q, :],
+                    start=(q == 0),
+                    stop=(q == Q - 1),
+                )
+            dxs[e, r] = work.tile([P, C], F32, name="dxs", bufs=4)
+            nc.scalar.activation(dxs[e, r][:], dx[:], COPY, scale=2.0)
+
+        def scatter(e, r):
+            nc.vector.tensor_copy(windows[r][:].indirect(offsets[:, e * 16 : (e + 1) * 16]), dxs[e, r][:])
+
+        scalar_copy = nc.scalar.copy
+        vector_copy = nc.vector.tensor_copy
+
+        def weights1(e, second=scalar_copy):
+            start_w1(e)
+            round_w1(e, 0, 0, K, scalar_copy)
+            round_w1(e, 1, 0, K, second)
+            quantise_w1(e)
+
+        def whole_back(e):
+            for r in range(R):
+                back(e, r)
+
+        def whole_scatter(e):
+            for r in range(R):
+                scatter(e, r)
+
+        for s0, s1 in PIECES:
+            gather(0, s0, s1)
+        for j in range(1, PACK):
+            gather(j, 0, S)
+        quantise_g(0, vector_copy)
+        quantise_w2(0, [scalar_copy, vector_copy])
+        quantise_g(1, scalar_copy)
+        hidden(0)
+        quantise_g(2, scalar_copy)
+        quantise_g(3, scalar_copy)
+        weights1(0)
+        whole_back(0)
+        for e in range(1, E - 1):
+            quantise_w2(e, [scalar_copy, vector_copy if e == 1 else scalar_copy])
+            hidden(e)
+            whole_scatter(e - 1)
+            weights1(e, vector_copy)
+            whole_back(e)
+        e = E - 1
+        quantise_w2(e, [scalar_copy, scalar_copy])
+        hidden(e)
+        whole_scatter(e - 1)
+        start_w1(e)
+        for r in range(R):
+            for q in range(Q):
+                round_w1(e, q, r * P, (r + 1) * P, scalar_copy)
+                quantise_w1_part(e, q, r * P, (r + 1) * P)
+            back(e, r)
+            scatter(e, r)
+
+        for r in range(R):
+            nc.sync.dma_start(out[r * P : (r + 1) * P, :], windows[r][:])

@@ -24,7 +24,6 @@ PACK = 4
 Q = H // (P * PACK)
 R = K // P
 HALF = 128
-PIECES = ((0, 128), (128, 512), (512, 1024))
 
 
 def tile_moe_bdx_mlp_relu2_kernel(tc, dyT, a, w2, w1, gate, offs, out):
@@ -36,7 +35,7 @@ def tile_moe_bdx_mlp_relu2_kernel(tc, dyT, a, w2, w1, gate, offs, out):
 
     with ExitStack() as ctx:
         held = ctx.enter_context(tc.tile_pool(name="held", bufs=1))
-        raw = ctx.enter_context(tc.tile_pool(name="raw", bufs=11))
+        raw = ctx.enter_context(tc.tile_pool(name="raw", bufs=6))
         work = ctx.enter_context(tc.tile_pool(name="work", bufs=2))
         psum = ctx.enter_context(tc.psum_pool(name="psum", bufs=1))
 
@@ -55,54 +54,49 @@ def tile_moe_bdx_mlp_relu2_kernel(tc, dyT, a, w2, w1, gate, offs, out):
             nc.gpsimd.memset(window[:], 0.0)
             windows.append(window)
 
-        def load(view, name, shape, tag="raw", bufs=None):
-            t = raw.tile(shape, F32, name=name, tag=tag) if bufs is None else raw.tile(shape, F32, name=name, tag=tag, bufs=bufs)
-            nc.sync.dma_start(t[:], view)
-            return t
-
         dy, w2_raw, w1_raw, a_raw = {}, {}, {}, {}
 
         def load_dy(j):
-            dy[j] = load(dy_rows[:, j, :], f"dy{j}", [P, T])
+            dy[j] = raw.tile([P, T], F32, name=f"dy{j}", tag="raw")
+            nc.sync.dma_start(dy[j][:], dy_rows[:, j, :])
 
-        def load_w2(e, halves=False):
-            w2_raw[e] = raw.tile([P, PACK, H], F32, name=f"w2raw{e}", tag="w2raw", bufs=3)
-            step = 512 if halves else H
-            for c in range(0, H, step):
-                nc.sync.dma_start(w2_raw[e][:, :, c : c + step], w2_rows[e, :, :, c : c + step])
+        def load_w2(e, c0, c1):
+            if c0 == 0:
+                w2_raw[e] = raw.tile([P, PACK, H], F32, name=f"w2raw{e}", tag="w2raw", bufs=3)
+            nc.sync.dma_start(w2_raw[e][:, :, c0:c1], w2_rows[e, :, :, c0:c1])
 
-        def load_w1(e, halves=False):
+        def load_w1(e):
             w1_raw[e] = raw.tile([P, Q, PACK, K], F32, name=f"w1raw{e}", tag="raw")
-            if halves:
-                for q in range(Q):
-                    nc.sync.dma_start(w1_raw[e][:, q], w1_rows[e, :, q])
-            else:
-                nc.sync.dma_start(w1_raw[e][:], w1_rows[e])
+            nc.sync.dma_start(w1_raw[e][:], w1_rows[e])
 
-        def load_a(h, q):
-            a_raw[h, q] = load(a_rows[q, :, :, h * 512 : (h + 1) * 512], f"araw{h}{q}", [P, PACK, 512])
+        def load_a(e, n, q):
+            both = held.tile([P, PACK, n * C], F32, name=f"araw{e}{q}")
+            nc.sync.dma_start(both[:], a_rows[q, :, :, e * C : (e + n) * C])
+            for x in range(n):
+                a_raw[e + x, q] = both[:, :, x * C : (x + 1) * C]
 
         load_dy(0)
-        for j in range(1, PACK):
-            load_dy(j)
-        load_w2(0)
-        load_w2(1)
-        load_a(0, 0)
-        load_a(0, 1)
+        load_dy(1)
+        load_dy(2)
+        load_w2(0, 0, H)
+        load_dy(3)
+        load_w2(1, 0, H)
+        load_a(0, 2, 0)
         load_w1(0)
+        load_a(0, 2, 1)
         load_w1(1)
-        load_w2(2)
-        load_w2(3)
-        load_a(1, 0)
-        load_a(1, 1)
+        load_w2(2, 0, H)
+        load_w2(3, 0, H)
+        load_a(2, 2, 0)
         load_w1(2)
-        load_w1(3, halves=True)
+        load_a(2, 2, 1)
+        load_w1(3)
 
         turned = psum.tile([P, P], F32, name="turned", tag="dx", bufs=2)
         nc.tensor.transpose(turned[:], gate_rows[:], identity[:])
         gate_cols = held.tile([P, S // P], F32, name="gate_cols")
         nc.scalar.copy(gate_cols[:], turned[:, 0 : S // P])
-        for s0, s1 in PIECES[1:]:
+        for s0, s1 in ((128, 512), (512, 1024)):
             spread = psum.tile([P, 512], F32, name="spread", tag="dx", bufs=2)
             for c in range(s0, s1, P):
                 nc.tensor.transpose(
@@ -113,7 +107,10 @@ def tile_moe_bdx_mlp_relu2_kernel(tc, dyT, a, w2, w1, gate, offs, out):
         g4 = held.tile([P, PACK, S], F32, name="g4")
         g_codes = held.tile([P, S], U32, name="g_codes", align_bytes=64)
         g_scales = held.tile([P, S], U8, name="g_scales", align_bytes=64)
-        w2_codes, w2_scales, w1_codes, w1_scales, da, dxs, vb = {}, {}, {}, {}, {}, {}, {}
+        w2_codes, w2_scales, w1_codes, w1_scales, wb, vb, db = {}, {}, {}, {}, {}, {}, {}
+        da_codes, da_scales, dx_banks, dxs = {}, {}, {}, {}
+        on_scalar = nc.scalar.copy
+        on_vector = nc.vector.tensor_copy
 
         def gather(j, s0, s1):
             nc.vector.tensor_tensor(
@@ -129,145 +126,186 @@ def tile_moe_bdx_mlp_relu2_kernel(tc, dyT, a, w2, w1, gate, offs, out):
             )
             nc.vector.quantize_mx(out=g_codes[:, cols].bitcast(FP8X4), scales=g_scales[:, cols], in_=gb[:])
 
-        def quantise_w2(e, copies):
-            w2_codes[e] = work.tile([P, H], U32, name="w2_codes", align_bytes=64)
-            w2_scales[e] = work.tile([P, H], U8, name="w2_scales", align_bytes=64)
-            for q in range(Q):
-                cols = slice(q * 512, (q + 1) * 512)
-                wb = work.tile([P, PACK * 512], BF16, name="wb", align_bytes=64, bufs=3)
-                copies[q](
-                    out=wb[:].rearrange("p (t m j) -> p m j t", t=PACK, j=PACK),
-                    in_=w2_raw[e][:, :, cols].rearrange("p j (m t) -> p m j t", t=PACK),
-                )
-                nc.vector.quantize_mx(out=w2_codes[e][:, cols].bitcast(FP8X4), scales=w2_scales[e][:, cols], in_=wb[:])
-
-        def start_w1(e):
-            w1_codes[e] = work.tile([P, Q, K], U32, name="w1_codes", align_bytes=64)
-            w1_scales[e] = work.tile([P, Q, K], U8, name="w1_scales", align_bytes=64)
-            vb[e] = work.tile([P, Q, K * PACK], BF16, name="vb", align_bytes=64)
-
-        def round_w1(e, q, c0, c1, copy):
+        def round_w2(e, q, h, copy):
+            if h == 0:
+                wb[e, q] = work.tile([P, PACK * 512], BF16, name="wb", align_bytes=64, bufs=3)
+            ms = slice(h * 64, (h + 1) * 64)
             copy(
-                out=vb[e][:, q, c0 * PACK : c1 * PACK].rearrange("p (c i t) -> p c t i", i=4, t=PACK),
-                in_=w1_raw[e][:, q, :, c0:c1].rearrange("p t (c i) -> p c t i", i=4),
+                out=wb[e, q][:].rearrange("p (t m j) -> p m j t", t=PACK, j=PACK)[:, ms],
+                in_=w2_raw[e][:, :, q * 512 : (q + 1) * 512].rearrange("p j (m t) -> p m j t", t=PACK)[:, ms],
+            )
+
+        def quantise_w2(e, q):
+            if q == 0:
+                w2_codes[e] = work.tile([P, H], U32, name="w2_codes", align_bytes=64, bufs=2)
+                w2_scales[e] = work.tile([P, H], U8, name="w2_scales", align_bytes=64, bufs=2)
+            cols = slice(q * 512, (q + 1) * 512)
+            nc.vector.quantize_mx(
+                out=w2_codes[e][:, cols].bitcast(FP8X4), scales=w2_scales[e][:, cols], in_=wb[e, q][:]
+            )
+
+        def round_w1(e, q, copy):
+            if q == 0:
+                vb[e] = work.tile([P, Q, K * PACK], BF16, name="vb", align_bytes=64)
+            copy(
+                out=vb[e][:, q].rearrange("p (c i t) -> p c t i", i=4, t=PACK),
+                in_=w1_raw[e][:, q].rearrange("p t (c i) -> p c t i", i=4),
             )
 
         def quantise_w1(e):
+            w1_codes[e] = work.tile([P, Q, K], U32, name="w1_codes", align_bytes=64)
+            w1_scales[e] = work.tile([P, Q, K], U8, name="w1_scales", align_bytes=64)
             nc.vector.quantize_mx(
                 out=w1_codes[e][:].rearrange("p q k -> p (q k)").bitcast(FP8X4),
                 scales=w1_scales[e][:].rearrange("p q k -> p (q k)"),
                 in_=vb[e][:].rearrange("p q k -> p (q k)"),
             )
 
-        def quantise_w1_part(e, q, c0, c1):
+        def hidden(e, q):
+            db[e, q] = work.tile([P, C, PACK], BF16, name="db", align_bytes=64, bufs=4)
+            for h in range(C // HALF):
+                dh = psum.tile([P, PACK, HALF], F32, name="dh", bufs=6)
+                s0 = e * C + h * HALF
+                for t in range(PACK):
+                    wc = slice(q * 512 + t * P, q * 512 + (t + 1) * P)
+                    nc.tensor.matmul_mx(
+                        out=dh[:, t, :],
+                        lhsT=w2_codes[e][:, wc].bitcast(FP8X4),
+                        lhsT_scale=w2_scales[e][:, wc],
+                        rhs=g_codes[:, s0 : s0 + HALF].bitcast(FP8X4),
+                        rhs_scale=g_scales[:, s0 : s0 + HALF],
+                        start=True,
+                        stop=True,
+                    )
+                nc.vector.scalar_tensor_tensor(
+                    out=db[e, q][:, h * HALF : (h + 1) * HALF, :],
+                    in0=a_raw[e, q][:, :, h * HALF : (h + 1) * HALF].rearrange("p t s -> p s t"),
+                    scalar=0.0,
+                    in1=dh[:].rearrange("p t s -> p s t"),
+                    op0=ALU.max,
+                    op1=ALU.mult,
+                )
+
+        def quantise_da(e, q):
+            if q == 0:
+                da_codes[e] = work.tile([P, Q, C], U32, name="da_codes", align_bytes=64)
+                da_scales[e] = work.tile([P, Q, C], U8, name="da_scales", align_bytes=64)
             nc.vector.quantize_mx(
-                out=w1_codes[e][:, q, c0:c1].bitcast(FP8X4),
-                scales=w1_scales[e][:, q, c0:c1],
-                in_=vb[e][:, q, c0 * PACK : c1 * PACK],
+                out=da_codes[e][:, q, :].bitcast(FP8X4),
+                scales=da_scales[e][:, q, :],
+                in_=db[e, q][:].rearrange("p s t -> p (s t)"),
             )
 
-        def hidden(e):
-            db = {}
-            for q in range(Q):
-                db[q] = work.tile([P, C, PACK], BF16, name="db", align_bytes=64, bufs=3)
-                for h in range(C // HALF):
-                    dh = psum.tile([P, PACK, HALF], F32, name="dh", bufs=6)
-                    s0 = e * C + h * HALF
-                    for t in range(PACK):
-                        wc = slice(q * 512 + t * P, q * 512 + (t + 1) * P)
-                        nc.tensor.matmul_mx(
-                            out=dh[:, t, :],
-                            lhsT=w2_codes[e][:, wc].bitcast(FP8X4),
-                            lhsT_scale=w2_scales[e][:, wc],
-                            rhs=g_codes[:, s0 : s0 + HALF].bitcast(FP8X4),
-                            rhs_scale=g_scales[:, s0 : s0 + HALF],
-                            start=True,
-                            stop=True,
-                        )
-                    ac = (e % 2) * C + h * HALF
-                    nc.vector.scalar_tensor_tensor(
-                        out=db[q][:, h * HALF : (h + 1) * HALF, :],
-                        in0=a_raw[e // 2, q][:, :, ac : ac + HALF].rearrange("p t s -> p s t"),
-                        scalar=0.0,
-                        in1=dh[:].rearrange("p t s -> p s t"),
-                        op0=ALU.max,
-                        op1=ALU.mult,
-                    )
-            codes = work.tile([P, Q, C], U32, name="da_codes", align_bytes=64)
-            scales = work.tile([P, Q, C], U8, name="da_scales", align_bytes=64)
-            for q in range(Q):
-                nc.vector.quantize_mx(
-                    out=codes[:, q, :].bitcast(FP8X4),
-                    scales=scales[:, q, :],
-                    in_=db[q][:].rearrange("p s t -> p (s t)"),
-                )
-            da[e] = (codes, scales)
-
         def back(e, r):
-            codes, scales = da[e]
-            dx = psum.tile([P, C], F32, name="dx", tag="dx", bufs=2)
+            dx_banks[e, r] = psum.tile([P, C], F32, name="dx", tag="dx", bufs=2)
             for q in range(Q):
                 nc.tensor.matmul_mx(
-                    out=dx[:],
+                    out=dx_banks[e, r][:],
                     lhsT=w1_codes[e][:, q, r * P : (r + 1) * P].bitcast(FP8X4),
                     lhsT_scale=w1_scales[e][:, q, r * P : (r + 1) * P],
-                    rhs=codes[:, q, :].bitcast(FP8X4),
-                    rhs_scale=scales[:, q, :],
+                    rhs=da_codes[e][:, q, :].bitcast(FP8X4),
+                    rhs_scale=da_scales[e][:, q, :],
                     start=(q == 0),
                     stop=(q == Q - 1),
                 )
-            dxs[e, r] = work.tile([P, C], F32, name="dxs", bufs=4)
-            nc.scalar.activation(dxs[e, r][:], dx[:], COPY, scale=2.0)
+
+        def leave(e, r, room=None):
+            if room is None:
+                own = work.tile([P, C], F32, name="dxs", bufs=4)
+                room = own[:]
+            dxs[e, r] = room
+            nc.scalar.activation(room, dx_banks[e, r][:], COPY, scale=2.0)
 
         def scatter(e, r):
-            nc.vector.tensor_copy(windows[r][:].indirect(offsets[:, e * 16 : (e + 1) * 16]), dxs[e, r][:])
+            nc.vector.tensor_copy(windows[r][:].indirect(offsets[:, e * 16 : (e + 1) * 16]), dxs[e, r])
 
-        scalar_copy = nc.scalar.copy
-        vector_copy = nc.vector.tensor_copy
-
-        def weights1(e, second=scalar_copy):
-            start_w1(e)
-            round_w1(e, 0, 0, K, scalar_copy)
-            round_w1(e, 1, 0, K, second)
-            quantise_w1(e)
-
-        def whole_back(e):
-            for r in range(R):
-                back(e, r)
-
-        def whole_scatter(e):
-            for r in range(R):
-                scatter(e, r)
-
-        for s0, s1 in PIECES:
-            gather(0, s0, s1)
-        for j in range(1, PACK):
-            gather(j, 0, S)
-        quantise_g(0, vector_copy)
-        quantise_w2(0, [scalar_copy, vector_copy])
-        quantise_g(1, scalar_copy)
-        hidden(0)
-        quantise_g(2, scalar_copy)
-        quantise_g(3, scalar_copy)
-        weights1(0)
-        whole_back(0)
-        for e in range(1, E - 1):
-            quantise_w2(e, [scalar_copy, vector_copy if e == 1 else scalar_copy])
-            hidden(e)
-            whole_scatter(e - 1)
-            weights1(e, vector_copy)
-            whole_back(e)
-        e = E - 1
-        quantise_w2(e, [scalar_copy, scalar_copy])
-        hidden(e)
-        whole_scatter(e - 1)
-        start_w1(e)
-        for r in range(R):
-            for q in range(Q):
-                round_w1(e, q, r * P, (r + 1) * P, scalar_copy)
-                quantise_w1_part(e, q, r * P, (r + 1) * P)
-            back(e, r)
-            scatter(e, r)
+        gather(0, 0, 128)
+        gather(0, 128, 512)
+        gather(0, 512, 1024)
+        gather(1, 0, 1024)
+        gather(2, 0, 1024)
+        gather(3, 0, 512)
+        quantise_g(0, on_scalar)
+        quantise_g(1, on_scalar)
+        gather(3, 512, 1024)
+        round_w2(0, 0, 0, on_scalar)
+        round_w2(0, 0, 1, on_scalar)
+        quantise_w2(0, 0)
+        round_w2(0, 1, 0, on_scalar)
+        round_w2(0, 1, 1, on_scalar)
+        quantise_w2(0, 1)
+        round_w2(1, 0, 0, on_scalar)
+        round_w2(1, 0, 1, on_scalar)
+        quantise_w2(1, 0)
+        round_w2(1, 1, 0, on_scalar)
+        round_w2(1, 1, 1, on_scalar)
+        quantise_w2(1, 1)
+        quantise_g(2, on_vector)
+        quantise_g(3, on_vector)
+        hidden(0, 0)
+        quantise_da(0, 0)
+        hidden(1, 0)
+        quantise_da(1, 0)
+        hidden(0, 1)
+        quantise_da(0, 1)
+        round_w1(0, 0, on_scalar)
+        round_w1(0, 1, on_scalar)
+        quantise_w1(0)
+        back(0, 0)
+        back(0, 1)
+        hidden(1, 1)
+        quantise_da(1, 1)
+        round_w1(1, 0, on_scalar)
+        round_w1(1, 1, on_scalar)
+        quantise_w1(1)
+        leave(0, 0)
+        scatter(0, 0)
+        leave(0, 1)
+        scatter(0, 1)
+        back(1, 0)
+        back(1, 1)
+        round_w2(2, 0, 0, on_scalar)
+        leave(1, 0, w2_raw[2][:, 2, 0 * C : 1 * C])
+        scatter(1, 0)
+        leave(1, 1, w2_raw[2][:, 3, 0 * C : 1 * C])
+        scatter(1, 1)
+        round_w2(2, 0, 1, on_scalar)
+        quantise_w2(2, 0)
+        round_w2(2, 1, 0, on_scalar)
+        round_w2(2, 1, 1, on_scalar)
+        quantise_w2(2, 1)
+        round_w2(3, 0, 0, on_scalar)
+        round_w2(3, 0, 1, on_scalar)
+        quantise_w2(3, 0)
+        round_w2(3, 1, 0, on_scalar)
+        round_w2(3, 1, 1, on_scalar)
+        quantise_w2(3, 1)
+        hidden(2, 0)
+        quantise_da(2, 0)
+        hidden(3, 0)
+        quantise_da(3, 0)
+        hidden(2, 1)
+        quantise_da(2, 1)
+        round_w1(2, 0, on_scalar)
+        round_w1(2, 1, on_scalar)
+        quantise_w1(2)
+        back(2, 0)
+        back(2, 1)
+        hidden(3, 1)
+        quantise_da(3, 1)
+        round_w1(3, 0, on_scalar)
+        round_w1(3, 1, on_scalar)
+        quantise_w1(3)
+        leave(2, 0, w1_raw[3][:, 0, 0, :])
+        leave(2, 1, w1_raw[3][:, 0, 1, :])
+        back(3, 0)
+        back(3, 1)
+        leave(3, 0)
+        leave(3, 1)
+        scatter(2, 0)
+        scatter(3, 0)
+        scatter(2, 1)
+        scatter(3, 1)
 
         for r in range(R):
             nc.sync.dma_start(out[r * P : (r + 1) * P, :], windows[r][:])

@@ -41,8 +41,6 @@ def tile_moe_bdx_mlp_relu2_kernel(tc, dyT, a, w2, w1, gate, offs, out):
 
         offsets = held.tile([P, S // 16], U16, name="offsets")
         gates = held.tile([P, S], F32, name="gates")
-        nc.sync.dma_start(gates[:, 0:P], gate[0:P, 0:P])
-        nc.sync.dma_start(offsets[:], offs)
         gate_rows = held.tile([P, P], F32, name="gate_rows")
         nc.scalar.dma_start(gate_rows[:], gate[0 : P * P // S, :].rearrange("r (b c) -> (r b) c", c=P))
         identity = held.tile([P, P], F32, name="identity")
@@ -76,10 +74,11 @@ def tile_moe_bdx_mlp_relu2_kernel(tc, dyT, a, w2, w1, gate, offs, out):
                 a_raw[e + x, q] = both[:, :, x * C : (x + 1) * C]
 
         load_dy(0)
+        nc.sync.dma_start(offsets[:], offs)
         load_dy(1)
         load_dy(2)
-        load_w2(0, 0, H)
         load_dy(3)
+        load_w2(0, 0, H)
         load_w2(1, 0, H)
         load_a(0, 2, 0)
         load_w1(0)
@@ -92,12 +91,12 @@ def tile_moe_bdx_mlp_relu2_kernel(tc, dyT, a, w2, w1, gate, offs, out):
         load_a(2, 2, 1)
         load_w1(3)
 
-        turned = psum.tile([P, P], F32, name="turned", tag="dx", bufs=2)
+        turned = psum.tile([P, P], F32, name="turned", tag="dx0")
         nc.tensor.transpose(turned[:], gate_rows[:], identity[:])
         gate_cols = held.tile([P, S // P], F32, name="gate_cols")
         nc.scalar.copy(gate_cols[:], turned[:, 0 : S // P])
-        for s0, s1 in ((128, 512), (512, 1024)):
-            spread = psum.tile([P, 512], F32, name="spread", tag="dx", bufs=2)
+        for s0, s1 in ((0, 512), (512, 1024)):
+            spread = psum.tile([P, 512], F32, name="spread", tag=f"dx{1 - s0 // 512}")
             for c in range(s0, s1, P):
                 nc.tensor.transpose(
                     spread[:, c - s0 : c - s0 + P], gate_cols[:, c // P : c // P + 1].to_broadcast([P, P]), identity[:]
@@ -113,16 +112,16 @@ def tile_moe_bdx_mlp_relu2_kernel(tc, dyT, a, w2, w1, gate, offs, out):
         on_vector = nc.vector.tensor_copy
 
         def gather(j, s0, s1):
-            nc.vector.tensor_tensor(
-                g4[:, j, s0:s1], dy[j][:].indirect(offsets[:, s0 // 16 : s1 // 16]), gates[:, s0:s1], ALU.mult
-            )
+            nc.vector.tensor_copy(g4[:, j, s0:s1], dy[j][:].indirect(offsets[:, s0 // 16 : s1 // 16]))
 
-        def quantise_g(e, copy):
+        def quantise_g(e):
             gb = work.tile([P, PACK * C], BF16, name="gb", align_bytes=64)
             cols = slice(e * C, (e + 1) * C)
-            copy(
-                out=gb[:].rearrange("p (c i j) -> p c j i", i=4, j=PACK),
-                in_=g4[:, :, cols].rearrange("p j (c i) -> p c j i", i=4),
+            nc.vector.tensor_tensor(
+                gb[:].rearrange("p (c i j) -> p c j i", i=4, j=PACK),
+                g4[:, :, cols].rearrange("p j (c i) -> p c j i", i=4),
+                gates[:, cols].rearrange("p (c o i) -> p c o i", o=1, i=4).to_broadcast([P, C // 4, PACK, 4]),
+                ALU.mult,
             )
             nc.vector.quantize_mx(out=g_codes[:, cols].bitcast(FP8X4), scales=g_scales[:, cols], in_=gb[:])
 
@@ -196,8 +195,8 @@ def tile_moe_bdx_mlp_relu2_kernel(tc, dyT, a, w2, w1, gate, offs, out):
                 in_=db[e, q][:].rearrange("p s t -> p (s t)"),
             )
 
-        def back(e, r):
-            dx_banks[e, r] = psum.tile([P, C], F32, name="dx", tag="dx", bufs=2)
+        def back(e, r, bank):
+            dx_banks[e, r] = psum.tile([P, C], F32, name="dx", tag=f"dx{bank}")
             for q in range(Q):
                 nc.tensor.matmul_mx(
                     out=dx_banks[e, r][:],
@@ -219,14 +218,12 @@ def tile_moe_bdx_mlp_relu2_kernel(tc, dyT, a, w2, w1, gate, offs, out):
         def scatter(e, r):
             nc.vector.tensor_copy(windows[r][:].indirect(offsets[:, e * 16 : (e + 1) * 16]), dxs[e, r])
 
-        gather(0, 0, 128)
-        gather(0, 128, 512)
-        gather(0, 512, 1024)
+        gather(0, 0, 1024)
         gather(1, 0, 1024)
         gather(2, 0, 1024)
         gather(3, 0, 512)
-        quantise_g(0, on_scalar)
-        quantise_g(1, on_scalar)
+        quantise_g(0)
+        quantise_g(1)
         gather(3, 512, 1024)
         round_w2(0, 0, 0, on_scalar)
         round_w2(0, 0, 1, on_scalar)
@@ -240,30 +237,30 @@ def tile_moe_bdx_mlp_relu2_kernel(tc, dyT, a, w2, w1, gate, offs, out):
         round_w2(1, 1, 0, on_scalar)
         round_w2(1, 1, 1, on_scalar)
         quantise_w2(1, 1)
-        quantise_g(2, on_vector)
-        quantise_g(3, on_vector)
+        quantise_g(2)
+        quantise_g(3)
         hidden(0, 0)
-        quantise_da(0, 0)
         hidden(1, 0)
+        quantise_da(0, 0)
         quantise_da(1, 0)
         hidden(0, 1)
-        quantise_da(0, 1)
         round_w1(0, 0, on_scalar)
         round_w1(0, 1, on_scalar)
         quantise_w1(0)
-        back(0, 0)
-        back(0, 1)
+        quantise_da(0, 1)
+        back(0, 0, 0)
+        back(0, 1, 1)
         hidden(1, 1)
-        quantise_da(1, 1)
         round_w1(1, 0, on_scalar)
         round_w1(1, 1, on_scalar)
         quantise_w1(1)
+        quantise_da(1, 1)
         leave(0, 0)
         scatter(0, 0)
         leave(0, 1)
         scatter(0, 1)
-        back(1, 0)
-        back(1, 1)
+        back(1, 0, 0)
+        back(1, 1, 1)
         round_w2(2, 0, 0, on_scalar)
         leave(1, 0, w2_raw[2][:, 2, 0 * C : 1 * C])
         scatter(1, 0)
@@ -281,25 +278,25 @@ def tile_moe_bdx_mlp_relu2_kernel(tc, dyT, a, w2, w1, gate, offs, out):
         round_w2(3, 1, 1, on_scalar)
         quantise_w2(3, 1)
         hidden(2, 0)
-        quantise_da(2, 0)
         hidden(3, 0)
+        quantise_da(2, 0)
         quantise_da(3, 0)
         hidden(2, 1)
-        quantise_da(2, 1)
         round_w1(2, 0, on_scalar)
         round_w1(2, 1, on_scalar)
         quantise_w1(2)
-        back(2, 0)
-        back(2, 1)
+        quantise_da(2, 1)
+        back(2, 0, 0)
         hidden(3, 1)
-        quantise_da(3, 1)
         round_w1(3, 0, on_scalar)
         round_w1(3, 1, on_scalar)
         quantise_w1(3)
+        quantise_da(3, 1)
         leave(2, 0, w1_raw[3][:, 0, 0, :])
+        back(2, 1, 1)
         leave(2, 1, w1_raw[3][:, 0, 1, :])
-        back(3, 0)
-        back(3, 1)
+        back(3, 0, 0)
+        back(3, 1, 1)
         leave(3, 0)
         leave(3, 1)
         scatter(2, 0)

@@ -86,10 +86,12 @@ def tile_moe_bdx_mlp_relu2_kernel(tc, dyT, a, w2, w1, gate, offs, out):
         load_w1(1)
         load_w2(2, 0, H)
         load_w2(3, 0, H)
-        load_a(2, 2, 0)
+        load_a(2, 1, 0)
+        load_a(2, 1, 1)
         load_w1(2)
-        load_a(2, 2, 1)
+        load_a(3, 1, 0)
         load_w1(3)
+        load_a(3, 1, 1)
 
         turned = psum.tile([P, P], F32, name="turned", tag="dx0")
         nc.tensor.transpose(turned[:], gate_rows[:], identity[:])
@@ -271,37 +273,37 @@ def tile_moe_bdx_mlp_relu2_kernel(tc, dyT, a, w2, w1, gate, offs, out):
         round_w2(2, 1, 0, on_scalar)
         round_w2(2, 1, 1, on_scalar)
         quantise_w2(2, 1)
+        hidden(2, 0)
+        hidden(2, 1)
+        quantise_da(2, 0)
+        quantise_da(2, 1)
         round_w2(3, 0, 0, on_scalar)
         round_w2(3, 0, 1, on_scalar)
         quantise_w2(3, 0)
         round_w2(3, 1, 0, on_scalar)
         round_w2(3, 1, 1, on_scalar)
         quantise_w2(3, 1)
-        hidden(2, 0)
-        hidden(3, 0)
-        quantise_da(2, 0)
-        quantise_da(3, 0)
-        hidden(2, 1)
         round_w1(2, 0, on_scalar)
         round_w1(2, 1, on_scalar)
         quantise_w1(2)
-        quantise_da(2, 1)
         back(2, 0, 0)
+        back(2, 1, 1)
+        hidden(3, 0)
         hidden(3, 1)
+        quantise_da(3, 0)
         round_w1(3, 0, on_scalar)
+        leave(2, 0, w1_raw[3][:, 0, 0, :])
+        leave(2, 1, w1_raw[3][:, 0, 1, :])
         round_w1(3, 1, on_scalar)
         quantise_w1(3)
         quantise_da(3, 1)
-        leave(2, 0, w1_raw[3][:, 0, 0, :])
-        back(2, 1, 1)
-        leave(2, 1, w1_raw[3][:, 0, 1, :])
         back(3, 0, 0)
         back(3, 1, 1)
         leave(3, 0)
         leave(3, 1)
         scatter(2, 0)
-        scatter(3, 0)
         scatter(2, 1)
+        scatter(3, 0)
         scatter(3, 1)
 
         for r in range(R):

@@ -42,7 +42,8 @@ def tile_moe_bdx_mlp_relu2_kernel(tc, dyT, a, w2, w1, gate, offs, out):
         offsets = held.tile([P, S // 16], U16, name="offsets")
         gates = held.tile([P, S], F32, name="gates")
         gate_rows = held.tile([P, P], F32, name="gate_rows")
-        nc.scalar.dma_start(gate_rows[:], gate[0 : P * P // S, :].rearrange("r (b c) -> (r b) c", c=P))
+        nc.vector.memset(gate_rows[:], 0.0)
+        nc.scalar.dma_start(gate_rows[0 : S // P, :], gate[0:1, :].rearrange("r (b c) -> (r b) c", c=P))
         identity = held.tile([P, P], F32, name="identity")
         make_identity(nc, identity[:])
 

@@ -53,6 +53,9 @@ def tile_moe_bdx_mlp_relu2_kernel(tc, dyT, a, w2, w1, gate, offs, out):
             nc.gpsimd.memset(window[:], 0.0)
             windows.append(window)
 
+        zeros = held.tile([P, HALF], F32, name="zeros")
+        nc.gpsimd.memset(zeros[:], 0.0)
+
         dy, w2_raw, w1_raw, a_raw = {}, {}, {}, {}
 
         def load_dy(j):
@@ -254,10 +257,10 @@ def tile_moe_bdx_mlp_relu2_kernel(tc, dyT, a, w2, w1, gate, offs, out):
         back(0, 0, 0)
         back(0, 1, 1)
         hidden(1, 1)
+        quantise_da(1, 1)
         round_w1(1, 0, on_scalar)
         round_w1(1, 1, on_scalar)
         quantise_w1(1)
-        quantise_da(1, 1)
         leave(0, 0)
         scatter(0, 0)
         leave(0, 1)
@@ -301,11 +304,11 @@ def tile_moe_bdx_mlp_relu2_kernel(tc, dyT, a, w2, w1, gate, offs, out):
         back(3, 0, 0)
         back(3, 1, 1)
         leave(3, 0)
-        leave(3, 1)
+        leave(3, 1, w1_raw[3][:, 0, 2, :])
         scatter(2, 0)
-        scatter(2, 1)
+        nc.vector.tensor_tensor(windows[1][:].indirect(offsets[:, 32:40]), dxs[2, 1][:, 0:HALF], zeros[:], ALU.add)
         scatter(3, 0)
-        scatter(3, 1)
+        nc.vector.tensor_copy(windows[1][:].indirect(offsets[:, 40:64]), w1_raw[3][:, 0, 1:3, :].rearrange("p t k -> p (t k)")[:, HALF:])
 
         for r in range(R):
             nc.sync.dma_start(out[r * P : (r + 1) * P, :], windows[r][:])

@@ -95,7 +95,10 @@ def tile_moe_bdx_mlp_relu2_kernel(tc, dyT, a, w2, w1, gate, offs, out):
         load_w1(2)
         load_a(3, 1, 0)
         load_w1(3)
-        load_a(3, 1, 1)
+        last_a = held.tile([P, PACK, C], F32, name="araw31")
+        a_raw[3, 1] = last_a[:]
+        for c0 in range(0, C, HALF):
+            nc.sync.dma_start(last_a[:, :, c0 : c0 + HALF], a_rows[1, :, :, 3 * C + c0 : 3 * C + c0 + HALF])
 
         turned = psum.tile([P, P], F32, name="turned", tag="dx0")
         nc.tensor.transpose(turned[:], gate_rows[:], identity[:])

@@ -21,7 +21,8 @@ COPY = mybir.ActivationFunctionType.Copy
 
 P = 128
 PACK = 4
-Q = H // (P * PACK)
+PASS = P * PACK
+Q = H // PASS
 R = K // P
 HALF = 128
 
@@ -42,7 +43,7 @@ def tile_moe_bdx_mlp_relu2_kernel(tc, dyT, a, w2, w1, gate, offs, out):
         offsets = held.tile([P, S // 16], U16, name="offsets")
         gates = held.tile([P, S], F32, name="gates")
         gate_rows = held.tile([P, P], F32, name="gate_rows")
-        nc.vector.memset(gate_rows[:], 0.0)
+        nc.gpsimd.memset(gate_rows[:], 0.0)
         nc.scalar.dma_start(gate_rows[0 : S // P, :], gate[0:1, :].rearrange("r (b c) -> (r b) c", c=P))
         identity = held.tile([P, P], F32, name="identity")
         make_identity(nc, identity[:])
@@ -50,7 +51,7 @@ def tile_moe_bdx_mlp_relu2_kernel(tc, dyT, a, w2, w1, gate, offs, out):
         windows = []
         for r in range(R):
             window = held.tile([P, T], F32, name=f"window{r}")
-            nc.gpsimd.memset(window[:], 0.0)
+            (nc.vector, nc.gpsimd)[r].memset(window[:], 0.0)
             windows.append(window)
 
         zeros = held.tile([P, HALF], F32, name="zeros")
@@ -62,43 +63,43 @@ def tile_moe_bdx_mlp_relu2_kernel(tc, dyT, a, w2, w1, gate, offs, out):
             dy[j] = raw.tile([P, T], F32, name=f"dy{j}", tag="raw")
             nc.sync.dma_start(dy[j][:], dy_rows[:, j, :])
 
-        def load_w2(e, c0, c1):
-            if c0 == 0:
-                w2_raw[e] = raw.tile([P, PACK, H], F32, name=f"w2raw{e}", tag="w2raw", bufs=3)
-            nc.sync.dma_start(w2_raw[e][:, :, c0:c1], w2_rows[e, :, :, c0:c1])
+        def load_w2(e):
+            whole = raw.tile([P, PACK, H], F32, name=f"w2raw{e}", tag="w2raw", bufs=3)
+            nc.sync.dma_start(whole[:], w2_rows[e])
+            for q in range(Q):
+                w2_raw[e, q] = whole[:, :, q * PASS : (q + 1) * PASS]
 
-        def load_w1(e):
+        def load_w1(e, pieces=1):
             w1_raw[e] = raw.tile([P, Q, PACK, K], F32, name=f"w1raw{e}", tag="raw")
-            nc.sync.dma_start(w1_raw[e][:], w1_rows[e])
+            for q0 in range(0, Q, Q // pieces):
+                nc.sync.dma_start(w1_raw[e][:, q0 : q0 + Q // pieces], w1_rows[e, :, q0 : q0 + Q // pieces])
 
-        def load_a(e, n, q):
+        def load_a(e, n, q, pieces=1):
             both = held.tile([P, PACK, n * C], F32, name=f"araw{e}{q}")
-            nc.sync.dma_start(both[:], a_rows[q, :, :, e * C : (e + n) * C])
+            width = n * C // pieces
+            for c0 in range(0, n * C, width):
+                nc.sync.dma_start(both[:, :, c0 : c0 + width], a_rows[q, :, :, e * C + c0 : e * C + c0 + width])
             for x in range(n):
                 a_raw[e + x, q] = both[:, :, x * C : (x + 1) * C]
 
         load_dy(0)
         nc.sync.dma_start(offsets[:], offs)
-        load_dy(1)
-        load_dy(2)
-        load_dy(3)
-        load_w2(0, 0, H)
-        load_w2(1, 0, H)
+        for j in range(1, PACK):
+            load_dy(j)
+        load_w2(0)
+        load_w2(1)
         load_a(0, 2, 0)
         load_w1(0)
         load_a(0, 2, 1)
         load_w1(1)
-        load_w2(2, 0, H)
-        load_w2(3, 0, H)
+        load_w2(2)
+        load_w2(3)
         load_a(2, 1, 0)
         load_a(2, 1, 1)
         load_w1(2)
         load_a(3, 1, 0)
-        load_w1(3)
-        last_a = held.tile([P, PACK, C], F32, name="araw31")
-        a_raw[3, 1] = last_a[:]
-        for c0 in range(0, C, HALF):
-            nc.sync.dma_start(last_a[:, :, c0 : c0 + HALF], a_rows[1, :, :, 3 * C + c0 : 3 * C + c0 + HALF])
+        load_a(3, 1, 1)
+        load_w1(3, pieces=2)
 
         turned = psum.tile([P, P], F32, name="turned", tag="dx0")
         nc.tensor.transpose(turned[:], gate_rows[:], identity[:])
@@ -113,73 +114,76 @@ def tile_moe_bdx_mlp_relu2_kernel(tc, dyT, a, w2, w1, gate, offs, out):
             nc.scalar.copy(gates[:, s0:s1], spread[:, 0 : s1 - s0])
 
         g4 = held.tile([P, PACK, S], F32, name="g4")
+        gb = held.tile([P, PACK * S], BF16, name="gb", align_bytes=64)
         g_codes = held.tile([P, S], U32, name="g_codes", align_bytes=64)
         g_scales = held.tile([P, S], U8, name="g_scales", align_bytes=64)
         w2_codes, w2_scales, w1_codes, w1_scales, wb, vb, db = {}, {}, {}, {}, {}, {}, {}
         da_codes, da_scales, dx_banks, dxs = {}, {}, {}, {}
-        on_scalar = nc.scalar.copy
-        on_vector = nc.vector.tensor_copy
 
         def gather(j, s0, s1):
             nc.vector.tensor_copy(g4[:, j, s0:s1], dy[j][:].indirect(offsets[:, s0 // 16 : s1 // 16]))
 
-        def quantise_g(e):
-            gb = work.tile([P, PACK * C], BF16, name="gb", align_bytes=64)
-            cols = slice(e * C, (e + 1) * C)
-            nc.vector.tensor_tensor(
-                gb[:].rearrange("p (c i j) -> p c j i", i=4, j=PACK),
-                g4[:, :, cols].rearrange("p j (c i) -> p c j i", i=4),
-                gates[:, cols].rearrange("p (c o i) -> p c o i", o=1, i=4).to_broadcast([P, C // 4, PACK, 4]),
+        def gated(s0, s1, eng=nc.vector):
+            eng.tensor_tensor(
+                gb[:, PACK * s0 : PACK * s1].rearrange("p (c i j) -> p c j i", i=4, j=PACK),
+                g4[:, :, s0:s1].rearrange("p j (c i) -> p c j i", i=4),
+                gates[:, s0:s1].rearrange("p (c o i) -> p c o i", o=1, i=4).to_broadcast([P, (s1 - s0) // 4, PACK, 4]),
                 ALU.mult,
             )
-            nc.vector.quantize_mx(out=g_codes[:, cols].bitcast(FP8X4), scales=g_scales[:, cols], in_=gb[:])
 
-        def round_w2(e, q, h, copy):
-            if h == 0:
-                wb[e, q] = work.tile([P, PACK * 512], BF16, name="wb", align_bytes=64, bufs=3)
-            ms = slice(h * 64, (h + 1) * 64)
-            copy(
-                out=wb[e, q][:].rearrange("p (t m j) -> p m j t", t=PACK, j=PACK)[:, ms],
-                in_=w2_raw[e][:, :, q * 512 : (q + 1) * 512].rearrange("p j (m t) -> p m j t", t=PACK)[:, ms],
+        def quantise_g(s0, s1):
+            nc.vector.quantize_mx(
+                out=g_codes[:, s0:s1].bitcast(FP8X4), scales=g_scales[:, s0:s1], in_=gb[:, PACK * s0 : PACK * s1]
             )
+
+        def round_w2(e, q, halves=(0, 1), copy=nc.scalar.copy):
+            if 0 in halves:
+                wb[e, q] = work.tile([P, PACK * PASS], BF16, name="wb", align_bytes=64, bufs=3)
+            for h in halves:
+                ms = slice(h * 64, (h + 1) * 64)
+                copy(
+                    out=wb[e, q][:].rearrange("p (t m j) -> p m j t", t=PACK, j=PACK)[:, ms],
+                    in_=w2_raw[e, q].rearrange("p j (m t) -> p m j t", t=PACK)[:, ms],
+                )
 
         def quantise_w2(e, q):
-            if q == 0:
-                w2_codes[e] = work.tile([P, H], U32, name="w2_codes", align_bytes=64, bufs=2)
-                w2_scales[e] = work.tile([P, H], U8, name="w2_scales", align_bytes=64, bufs=2)
-            cols = slice(q * 512, (q + 1) * 512)
-            nc.vector.quantize_mx(
-                out=w2_codes[e][:, cols].bitcast(FP8X4), scales=w2_scales[e][:, cols], in_=wb[e, q][:]
-            )
+            w2_codes[e, q] = work.tile([P, PASS], U32, name="w2_codes", align_bytes=64, bufs=4)
+            w2_scales[e, q] = work.tile([P, PASS], U8, name="w2_scales", align_bytes=64, bufs=4)
+            nc.vector.quantize_mx(out=w2_codes[e, q][:].bitcast(FP8X4), scales=w2_scales[e, q][:], in_=wb[e, q][:])
 
-        def round_w1(e, q, copy):
-            if q == 0:
+        def round_w1(e, passes=(0, 1)):
+            if 0 in passes:
                 vb[e] = work.tile([P, Q, K * PACK], BF16, name="vb", align_bytes=64)
-            copy(
-                out=vb[e][:, q].rearrange("p (c i t) -> p c t i", i=4, t=PACK),
-                in_=w1_raw[e][:, q].rearrange("p t (c i) -> p c t i", i=4),
-            )
+            for q in passes:
+                nc.scalar.copy(
+                    out=vb[e][:, q].rearrange("p (c i t) -> p c t i", i=4, t=PACK),
+                    in_=w1_raw[e][:, q].rearrange("p t (c i) -> p c t i", i=4),
+                )
 
-        def quantise_w1(e):
-            w1_codes[e] = work.tile([P, Q, K], U32, name="w1_codes", align_bytes=64)
-            w1_scales[e] = work.tile([P, Q, K], U8, name="w1_scales", align_bytes=64)
+        def quantise_w1(e, q0=0, q1=Q):
+            if q0 == 0:
+                w1_codes[e] = work.tile([P, Q, K], U32, name="w1_codes", align_bytes=64)
+                w1_scales[e] = work.tile([P, Q, K], U8, name="w1_scales", align_bytes=64)
             nc.vector.quantize_mx(
-                out=w1_codes[e][:].rearrange("p q k -> p (q k)").bitcast(FP8X4),
-                scales=w1_scales[e][:].rearrange("p q k -> p (q k)"),
-                in_=vb[e][:].rearrange("p q k -> p (q k)"),
+                out=w1_codes[e][:, q0:q1].rearrange("p q k -> p (q k)").bitcast(FP8X4),
+                scales=w1_scales[e][:, q0:q1].rearrange("p q k -> p (q k)"),
+                in_=vb[e][:, q0:q1].rearrange("p q k -> p (q k)"),
             )
 
-        def hidden(e, q):
-            db[e, q] = work.tile([P, C, PACK], BF16, name="db", align_bytes=64, bufs=4)
+        def hidden(e, q, room=None):
+            if room is None:
+                own = work.tile([P, C, PACK], BF16, name="db", align_bytes=64, bufs=4)
+                room = own[:]
+            db[e, q] = room
             for h in range(C // HALF):
                 dh = psum.tile([P, PACK, HALF], F32, name="dh", bufs=6)
                 s0 = e * C + h * HALF
                 for t in range(PACK):
-                    wc = slice(q * 512 + t * P, q * 512 + (t + 1) * P)
+                    wc = slice(t * P, (t + 1) * P)
                     nc.tensor.matmul_mx(
                         out=dh[:, t, :],
-                        lhsT=w2_codes[e][:, wc].bitcast(FP8X4),
-                        lhsT_scale=w2_scales[e][:, wc],
+                        lhsT=w2_codes[e, q][:, wc].bitcast(FP8X4),
+                        lhsT_scale=w2_scales[e, q][:, wc],
                         rhs=g_codes[:, s0 : s0 + HALF].bitcast(FP8X4),
                         rhs_scale=g_scales[:, s0 : s0 + HALF],
                         start=True,
@@ -201,11 +205,23 @@ def tile_moe_bdx_mlp_relu2_kernel(tc, dyT, a, w2, w1, gate, offs, out):
             nc.vector.quantize_mx(
                 out=da_codes[e][:, q, :].bitcast(FP8X4),
                 scales=da_scales[e][:, q, :],
-                in_=db[e, q][:].rearrange("p s t -> p (s t)"),
+                in_=db[e, q].rearrange("p s t -> p (s t)"),
             )
 
-        def back(e, r, bank):
-            dx_banks[e, r] = psum.tile([P, C], F32, name="dx", tag=f"dx{bank}")
+        def hidden_both(e):
+            both = work.tile([P, Q * C, PACK], BF16, name="dboth", align_bytes=64, bufs=1)
+            for q in range(Q):
+                hidden(e, q, both[:, q * C : (q + 1) * C, :])
+            da_codes[e] = work.tile([P, Q, C], U32, name="da_codes", align_bytes=64)
+            da_scales[e] = work.tile([P, Q, C], U8, name="da_scales", align_bytes=64)
+            nc.vector.quantize_mx(
+                out=da_codes[e][:].rearrange("p q s -> p (q s)").bitcast(FP8X4),
+                scales=da_scales[e][:].rearrange("p q s -> p (q s)"),
+                in_=both[:].rearrange("p s t -> p (s t)"),
+            )
+
+        def back(e, r):
+            dx_banks[e, r] = psum.tile([P, C], F32, name="dx", tag=f"dx{r}")
             for q in range(Q):
                 nc.tensor.matmul_mx(
                     out=dx_banks[e, r][:],
@@ -227,85 +243,75 @@ def tile_moe_bdx_mlp_relu2_kernel(tc, dyT, a, w2, w1, gate, offs, out):
         def scatter(e, r):
             nc.vector.tensor_copy(windows[r][:].indirect(offsets[:, e * 16 : (e + 1) * 16]), dxs[e, r])
 
-        gather(0, 0, 1024)
-        gather(1, 0, 1024)
-        gather(2, 0, 1024)
-        gather(3, 0, 512)
-        quantise_g(0)
-        quantise_g(1)
-        gather(3, 512, 1024)
-        round_w2(0, 0, 0, on_scalar)
-        round_w2(0, 0, 1, on_scalar)
-        quantise_w2(0, 0)
-        round_w2(0, 1, 0, on_scalar)
-        round_w2(0, 1, 1, on_scalar)
-        quantise_w2(0, 1)
-        round_w2(1, 0, 0, on_scalar)
-        round_w2(1, 0, 1, on_scalar)
-        quantise_w2(1, 0)
-        round_w2(1, 1, 0, on_scalar)
-        round_w2(1, 1, 1, on_scalar)
-        quantise_w2(1, 1)
-        quantise_g(2)
-        quantise_g(3)
+        for j in range(PACK - 1):
+            gather(j, 0, S)
+        gather(3, 0, 2 * C)
+        gated(0, C)
+        quantise_g(0, C)
+        gated(C, 2 * C)
+        quantise_g(C, 2 * C)
+        gather(3, 2 * C, S)
+        for e in (0, 1):
+            for q in range(Q):
+                round_w2(e, q)
+                quantise_w2(e, q)
+        gated(2 * C, 3 * C)
+        quantise_g(2 * C, 3 * C)
+        gated(3 * C, S)
+        quantise_g(3 * C, S)
         hidden(0, 0)
         hidden(1, 0)
         quantise_da(0, 0)
         quantise_da(1, 0)
         hidden(0, 1)
-        round_w1(0, 0, on_scalar)
-        round_w1(0, 1, on_scalar)
+        round_w1(0)
         quantise_w1(0)
         quantise_da(0, 1)
-        back(0, 0, 0)
-        back(0, 1, 1)
+        back(0, 0)
+        back(0, 1)
         hidden(1, 1)
         quantise_da(1, 1)
-        round_w1(1, 0, on_scalar)
-        round_w1(1, 1, on_scalar)
+        round_w1(1)
         quantise_w1(1)
         leave(0, 0)
         scatter(0, 0)
         leave(0, 1)
         scatter(0, 1)
-        back(1, 0, 0)
-        back(1, 1, 1)
-        round_w2(2, 0, 0, on_scalar)
-        leave(1, 0, w2_raw[2][:, 2, 0 * C : 1 * C])
+        back(1, 0)
+        back(1, 1)
+        leave(1, 0)
         scatter(1, 0)
-        leave(1, 1, w2_raw[2][:, 3, 0 * C : 1 * C])
+        round_w2(2, 0, (0,))
+        leave(1, 1, w2_raw[2, 0][:, 3, 0:C])
         scatter(1, 1)
-        round_w2(2, 0, 1, on_scalar)
+        round_w2(2, 0, (1,))
         quantise_w2(2, 0)
-        round_w2(2, 1, 0, on_scalar)
-        round_w2(2, 1, 1, on_scalar)
+        round_w2(2, 1)
         quantise_w2(2, 1)
         hidden(2, 0)
+        round_w2(3, 0)
+        quantise_w2(3, 0)
         hidden(2, 1)
         quantise_da(2, 0)
         quantise_da(2, 1)
-        round_w2(3, 0, 0, on_scalar)
-        round_w2(3, 0, 1, on_scalar)
-        quantise_w2(3, 0)
-        round_w2(3, 1, 0, on_scalar)
-        round_w2(3, 1, 1, on_scalar)
+        round_w2(3, 1)
         quantise_w2(3, 1)
-        round_w1(2, 0, on_scalar)
-        round_w1(2, 1, on_scalar)
+        round_w1(2)
         quantise_w1(2)
-        back(2, 0, 0)
-        back(2, 1, 1)
+        back(2, 0)
+        back(2, 1)
         hidden(3, 0)
         hidden(3, 1)
         quantise_da(3, 0)
-        round_w1(3, 0, on_scalar)
+        quantise_da(3, 1)
+        round_w1(3, (0,))
+        quantise_w1(3, 0, 1)
         leave(2, 0, w1_raw[3][:, 0, 0, :])
         leave(2, 1, w1_raw[3][:, 0, 1, :])
-        round_w1(3, 1, on_scalar)
-        quantise_w1(3)
-        quantise_da(3, 1)
-        back(3, 0, 0)
-        back(3, 1, 1)
+        round_w1(3, (1,))
+        quantise_w1(3, 1, 2)
+        back(3, 0)
+        back(3, 1)
         leave(3, 0)
         leave(3, 1, w1_raw[3][:, 0, 2, :])
         scatter(2, 0)

@@ -50,7 +50,7 @@ def tile_moe_bdx_mlp_relu2_kernel(tc, dyT, a, w2, w1, gate, offs, out):
 
         windows = []
         for r in range(R):
-            window = held.tile([P, T], F32, name=f"window{r}")
+            window = held.tile([P, T], F32, name=f"window{r}", align_bytes=256)
             (nc.vector, nc.gpsimd)[r].memset(window[:], 0.0)
             windows.append(window)
 
@@ -60,22 +60,22 @@ def tile_moe_bdx_mlp_relu2_kernel(tc, dyT, a, w2, w1, gate, offs, out):
         dy, w2_raw, w1_raw, a_raw = {}, {}, {}, {}
 
         def load_dy(j):
-            dy[j] = raw.tile([P, T], F32, name=f"dy{j}", tag="raw")
+            dy[j] = raw.tile([P, T], F32, name=f"dy{j}", tag="raw", align_bytes=256)
             nc.sync.dma_start(dy[j][:], dy_rows[:, j, :])
 
         def load_w2(e):
-            whole = raw.tile([P, PACK, H], F32, name=f"w2raw{e}", tag="w2raw", bufs=3)
+            whole = raw.tile([P, PACK, H], F32, name=f"w2raw{e}", tag="w2raw", bufs=3, align_bytes=256)
             nc.sync.dma_start(whole[:], w2_rows[e])
             for q in range(Q):
                 w2_raw[e, q] = whole[:, :, q * PASS : (q + 1) * PASS]
 
         def load_w1(e, pieces=1):
-            w1_raw[e] = raw.tile([P, Q, PACK, K], F32, name=f"w1raw{e}", tag="raw")
+            w1_raw[e] = raw.tile([P, Q, PACK, K], F32, name=f"w1raw{e}", tag="raw", align_bytes=256)
             for q0 in range(0, Q, Q // pieces):
                 nc.sync.dma_start(w1_raw[e][:, q0 : q0 + Q // pieces], w1_rows[e, :, q0 : q0 + Q // pieces])
 
         def load_a(e, n, q, pieces=1):
-            both = held.tile([P, PACK, n * C], F32, name=f"araw{e}{q}")
+            both = held.tile([P, PACK, n * C], F32, name=f"araw{e}{q}", align_bytes=256)
             width = n * C // pieces
             for c0 in range(0, n * C, width):
                 nc.sync.dma_start(both[:, :, c0 : c0 + width], a_rows[q, :, :, e * C + c0 : e * C + c0 + width])

@@ -91,7 +91,7 @@ def tile_moe_bdx_mlp_relu2_kernel(tc, dyT, a, w2, w1, gate, offs, out):
         load_a(0, 2, 0)
         load_w1(0)
         load_a(0, 2, 1)
-        load_w1(1)
+        load_w1(1, pieces=2)
         load_w2(2)
         load_w2(3)
         load_a(2, 1, 0)
@@ -146,28 +146,42 @@ def tile_moe_bdx_mlp_relu2_kernel(tc, dyT, a, w2, w1, gate, offs, out):
                     in_=w2_raw[e, q].rearrange("p j (m t) -> p m j t", t=PACK)[:, ms],
                 )
 
+        def round_w2_planes(e, q, t0, copy):
+            if t0 == 0:
+                wb[e, q] = work.tile([P, PACK * PASS], BF16, name="wb", align_bytes=64, bufs=3)
+            copy(
+                wb[e, q][:].rearrange("p (t m j) -> p t m j", t=PACK, j=PACK)[:, t0 : t0 + 2],
+                w2_raw[e, q].rearrange("p j (m t) -> p t m j", t=PACK)[:, t0 : t0 + 2],
+            )
+
+        def on_gpsimd(rounded, values):
+            nc.gpsimd.tensor_scalar(rounded, values, 1.0, 0.0, ALU.mult, ALU.add)
+
+        def on_scalar(rounded, values):
+            nc.scalar.copy(rounded.rearrange("p t m j -> p m j t"), values.rearrange("p t m j -> p m j t"))
+
         def quantise_w2(e, q):
             w2_codes[e, q] = work.tile([P, PASS], U32, name="w2_codes", align_bytes=64, bufs=4)
             w2_scales[e, q] = work.tile([P, PASS], U8, name="w2_scales", align_bytes=64, bufs=4)
             nc.vector.quantize_mx(out=w2_codes[e, q][:].bitcast(FP8X4), scales=w2_scales[e, q][:], in_=wb[e, q][:])
 
-        def round_w1(e, passes=(0, 1)):
+        def round_w1(e, passes=(0, 1), k0=0, k1=K):
             if 0 in passes:
                 vb[e] = work.tile([P, Q, K * PACK], BF16, name="vb", align_bytes=64)
             for q in passes:
                 nc.scalar.copy(
-                    out=vb[e][:, q].rearrange("p (c i t) -> p c t i", i=4, t=PACK),
-                    in_=w1_raw[e][:, q].rearrange("p t (c i) -> p c t i", i=4),
+                    out=vb[e][:, q, PACK * k0 : PACK * k1].rearrange("p (c i t) -> p c t i", i=4, t=PACK),
+                    in_=w1_raw[e][:, q, :, k0:k1].rearrange("p t (c i) -> p c t i", i=4),
                 )
 
-        def quantise_w1(e, q0=0, q1=Q):
-            if q0 == 0:
+        def quantise_w1(e, c0=0, c1=Q * K):
+            if c0 == 0:
                 w1_codes[e] = work.tile([P, Q, K], U32, name="w1_codes", align_bytes=64)
                 w1_scales[e] = work.tile([P, Q, K], U8, name="w1_scales", align_bytes=64)
             nc.vector.quantize_mx(
-                out=w1_codes[e][:, q0:q1].rearrange("p q k -> p (q k)").bitcast(FP8X4),
-                scales=w1_scales[e][:, q0:q1].rearrange("p q k -> p (q k)"),
-                in_=vb[e][:, q0:q1].rearrange("p q k -> p (q k)"),
+                out=w1_codes[e][:].rearrange("p q k -> p (q k)")[:, c0:c1].bitcast(FP8X4),
+                scales=w1_scales[e][:].rearrange("p q k -> p (q k)")[:, c0:c1],
+                in_=vb[e][:].rearrange("p q k -> p (q k)")[:, PACK * c0 : PACK * c1],
             )
 
         def hidden(e, q, room=None):
@@ -253,7 +267,7 @@ def tile_moe_bdx_mlp_relu2_kernel(tc, dyT, a, w2, w1, gate, offs, out):
         gather(3, 2 * C, S)
         for e in (0, 1):
             for q in range(Q):
-                round_w2(e, q)
+                round_w2(e, q, copy=nc.vector.tensor_copy if (e, q) == (1, 0) else nc.scalar.copy)
                 quantise_w2(e, q)
         gated(2 * C, 3 * C)
         quantise_g(2 * C, 3 * C)
@@ -270,9 +284,11 @@ def tile_moe_bdx_mlp_relu2_kernel(tc, dyT, a, w2, w1, gate, offs, out):
         back(0, 0)
         back(0, 1)
         hidden(1, 1)
+        round_w1(1, (0,))
+        quantise_w1(1, 0, K)
         quantise_da(1, 1)
-        round_w1(1)
-        quantise_w1(1)
+        round_w1(1, (1,))
+        quantise_w1(1, K, 2 * K)
         leave(0, 0)
         scatter(0, 0)
         leave(0, 1)
@@ -281,12 +297,12 @@ def tile_moe_bdx_mlp_relu2_kernel(tc, dyT, a, w2, w1, gate, offs, out):
         back(1, 1)
         leave(1, 0)
         scatter(1, 0)
-        round_w2(2, 0, (0,))
-        leave(1, 1, w2_raw[2, 0][:, 3, 0:C])
-        scatter(1, 1)
-        round_w2(2, 0, (1,))
+        round_w2(2, 0)
         quantise_w2(2, 0)
-        round_w2(2, 1)
+        leave(1, 1, w2_raw[2, 0][:, 3, C : 2 * C])
+        scatter(1, 1)
+        round_w2_planes(2, 1, 0, on_gpsimd)
+        round_w2_planes(2, 1, 2, on_scalar)
         quantise_w2(2, 1)
         hidden(2, 0)
         round_w2(3, 0)
@@ -305,13 +321,13 @@ def tile_moe_bdx_mlp_relu2_kernel(tc, dyT, a, w2, w1, gate, offs, out):
         quantise_da(3, 0)
         quantise_da(3, 1)
         round_w1(3, (0,))
-        quantise_w1(3, 0, 1)
+        quantise_w1(3, 0, K)
         leave(2, 0, w1_raw[3][:, 0, 0, :])
         leave(2, 1, w1_raw[3][:, 0, 1, :])
-        round_w1(3, (1,))
-        quantise_w1(3, 1, 2)
-        back(3, 0)
-        back(3, 1)
+        for r in range(R):
+            round_w1(3, (1,), r * P, (r + 1) * P)
+            quantise_w1(3, K + r * P, K + (r + 1) * P)
+            back(3, r)
         leave(3, 0)
         leave(3, 1, w1_raw[3][:, 0, 2, :])
         scatter(2, 0)

@@ -267,7 +267,8 @@ def tile_moe_bdx_mlp_relu2_kernel(tc, dyT, a, w2, w1, gate, offs, out):
         gather(3, 2 * C, S)
         for e in (0, 1):
             for q in range(Q):
-                round_w2(e, q, copy=nc.vector.tensor_copy if (e, q) == (1, 0) else nc.scalar.copy)
+                for h in (0, 1):
+                    round_w2(e, q, (h,), nc.vector.tensor_copy if (e, q, h) == (1, 0, 0) else nc.scalar.copy)
                 quantise_w2(e, q)
         gated(2 * C, 3 * C)
         quantise_g(2 * C, 3 * C)
@@ -277,9 +278,11 @@ def tile_moe_bdx_mlp_relu2_kernel(tc, dyT, a, w2, w1, gate, offs, out):
         hidden(1, 0)
         quantise_da(0, 0)
         quantise_da(1, 0)
+        round_w1(0, (0,))
+        quantise_w1(0, 0, K)
         hidden(0, 1)
-        round_w1(0)
-        quantise_w1(0)
+        round_w1(0, (1,))
+        quantise_w1(0, K, 2 * K)
         quantise_da(0, 1)
         back(0, 0)
         back(0, 1)
@@ -299,7 +302,7 @@ def tile_moe_bdx_mlp_relu2_kernel(tc, dyT, a, w2, w1, gate, offs, out):
         scatter(1, 0)
         round_w2(2, 0)
         quantise_w2(2, 0)
-        leave(1, 1, w2_raw[2, 0][:, 3, C : 2 * C])
+        leave(1, 1, w2_raw[2, 0][:, 3, 0:C])
         scatter(1, 1)
         round_w2_planes(2, 1, 0, on_gpsimd)
         round_w2_planes(2, 1, 2, on_scalar)
@@ -322,11 +325,10 @@ def tile_moe_bdx_mlp_relu2_kernel(tc, dyT, a, w2, w1, gate, offs, out):
         quantise_da(3, 1)
         round_w1(3, (0,))
         quantise_w1(3, 0, K)
-        leave(2, 0, w1_raw[3][:, 0, 0, :])
-        leave(2, 1, w1_raw[3][:, 0, 1, :])
         for r in range(R):
             round_w1(3, (1,), r * P, (r + 1) * P)
             quantise_w1(3, K + r * P, K + (r + 1) * P)
+            leave(2, r, w1_raw[3][:, 0, r, :])
             back(3, r)
         leave(3, 0)
         leave(3, 1, w1_raw[3][:, 0, 2, :])

@@ -54,9 +54,6 @@ def tile_moe_bdx_mlp_relu2_kernel(tc, dyT, a, w2, w1, gate, offs, out):
             (nc.vector, nc.gpsimd)[r].memset(window[:], 0.0)
             windows.append(window)
 
-        zeros = held.tile([P, HALF], F32, name="zeros")
-        nc.gpsimd.memset(zeros[:], 0.0)
-
         dy, w2_raw, w1_raw, a_raw = {}, {}, {}, {}
 
         def load_dy(j):
@@ -257,6 +254,9 @@ def tile_moe_bdx_mlp_relu2_kernel(tc, dyT, a, w2, w1, gate, offs, out):
         def scatter(e, r):
             nc.vector.tensor_copy(windows[r][:].indirect(offsets[:, e * 16 : (e + 1) * 16]), dxs[e, r])
 
+        def scatter_on_scalar(e, r):
+            nc.scalar.activation(windows[r][:].indirect(offsets[:, e * 16 : (e + 1) * 16]), dxs[e, r], COPY)
+
         for j in range(PACK - 1):
             gather(j, 0, S)
         gather(3, 0, 2 * C)
@@ -331,11 +331,11 @@ def tile_moe_bdx_mlp_relu2_kernel(tc, dyT, a, w2, w1, gate, offs, out):
             leave(2, r, w1_raw[3][:, 0, r, :])
             back(3, r)
         leave(3, 0)
-        leave(3, 1, w1_raw[3][:, 0, 2, :])
         scatter(2, 0)
-        nc.vector.tensor_tensor(windows[1][:].indirect(offsets[:, 32:40]), dxs[2, 1][:, 0:HALF], zeros[:], ALU.add)
         scatter(3, 0)
-        nc.vector.tensor_copy(windows[1][:].indirect(offsets[:, 40:64]), w1_raw[3][:, 0, 1:3, :].rearrange("p t k -> p (t k)")[:, HALF:])
+        scatter_on_scalar(2, 1)
+        leave(3, 1)
+        scatter_on_scalar(3, 1)
 
         for r in range(R):
             nc.sync.dma_start(out[r * P : (r + 1) * P, :], windows[r][:])

from contextlib import ExitStack

import concourse.mybir as mybir
from concourse.masks import make_identity

K, T, E, C, H, N = 256, 2048, 4, 256, 1024, 512
S = E * C

FLOPS = 2 * S * H * (N + K)
BYTES = 4 * (N * T + H * S + E * N * H + E * H * K + S + K * T) + 2 * 128 * (S // 16)

F32 = mybir.dt.float32
BF16 = mybir.dt.bfloat16
U32 = mybir.dt.uint32
U16 = mybir.dt.uint16
U8 = mybir.dt.uint8
FP8X4 = mybir.dt.float8_e4m3fn_x4

ALU = mybir.AluOpType
COPY = mybir.ActivationFunctionType.Copy

P = 128
PACK = 4
PASS = P * PACK
Q = H // PASS
R = K // P
HALF = 128


def tile_moe_bdx_mlp_relu2_kernel(tc, dyT, a, w2, w1, gate, offs, out):
    nc = tc.nc
    dy_rows = dyT.rearrange("(p j) t -> p j t", j=PACK)
    a_rows = a.rearrange("(q p t) s -> q p t s", q=Q, t=PACK)
    w2_rows = w2.rearrange("e (p j) i -> e p j i", j=PACK)
    w1_rows = w1.rearrange("e (q p t) k -> e p q t k", q=Q, t=PACK)

    with ExitStack() as ctx:
        held = ctx.enter_context(tc.tile_pool(name="held", bufs=1))
        raw = ctx.enter_context(tc.tile_pool(name="raw", bufs=6))
        work = ctx.enter_context(tc.tile_pool(name="work", bufs=2))
        psum = ctx.enter_context(tc.psum_pool(name="psum", bufs=1))

        offsets = held.tile([P, S // 16], U16, name="offsets")
        gates = held.tile([P, S], F32, name="gates")
        gate_rows = held.tile([P, P], F32, name="gate_rows")
        nc.gpsimd.memset(gate_rows[:], 0.0)
        nc.scalar.dma_start(gate_rows[0 : S // P, :], gate[0:1, :].rearrange("r (b c) -> (r b) c", c=P))
        identity = held.tile([P, P], F32, name="identity")
        make_identity(nc, identity[:])

        windows = []
        for r in range(R):
            window = held.tile([P, T], F32, name=f"window{r}", align_bytes=256)
            (nc.vector, nc.gpsimd)[r].memset(window[:], 0.0)
            windows.append(window)

        dy, w2_raw, w1_raw, a_raw = {}, {}, {}, {}

        def load_dy(j):
            dy[j] = raw.tile([P, T], F32, name=f"dy{j}", tag="raw", align_bytes=256)
            nc.sync.dma_start(dy[j][:], dy_rows[:, j, :])

        def load_w2(e):
            whole = raw.tile([P, PACK, H], F32, name=f"w2raw{e}", tag="w2raw", bufs=3, align_bytes=256)
            nc.sync.dma_start(whole[:], w2_rows[e])
            for q in range(Q):
                w2_raw[e, q] = whole[:, :, q * PASS : (q + 1) * PASS]

        def load_w1(e, pieces=1):
            w1_raw[e] = raw.tile([P, Q, PACK, K], F32, name=f"w1raw{e}", tag="raw", align_bytes=256)
            for q0 in range(0, Q, Q // pieces):
                nc.sync.dma_start(w1_raw[e][:, q0 : q0 + Q // pieces], w1_rows[e, :, q0 : q0 + Q // pieces])

        def load_a(e, n, q, pieces=1):
            both = held.tile([P, PACK, n * C], F32, name=f"araw{e}{q}", align_bytes=256)
            width = n * C // pieces
            for c0 in range(0, n * C, width):
                nc.sync.dma_start(both[:, :, c0 : c0 + width], a_rows[q, :, :, e * C + c0 : e * C + c0 + width])
            for x in range(n):
                a_raw[e + x, q] = both[:, :, x * C : (x + 1) * C]

        load_dy(0)
        nc.sync.dma_start(offsets[:], offs)
        for j in range(1, PACK):
            load_dy(j)
        load_w2(0)
        load_w2(1)
        load_a(0, 2, 0)
        load_w1(0)
        load_a(0, 2, 1)
        load_w1(1, pieces=2)
        load_w2(2)
        load_w2(3)
        load_a(2, 1, 0)
        load_a(2, 1, 1)
        load_w1(2)
        load_a(3, 1, 0)
        load_a(3, 1, 1)
        load_w1(3, pieces=2)

        turned = psum.tile([P, P], F32, name="turned", tag="dx0")
        nc.tensor.transpose(turned[:], gate_rows[:], identity[:])
        gate_cols = held.tile([P, S // P], F32, name="gate_cols")
        nc.scalar.copy(gate_cols[:], turned[:, 0 : S // P])
        for s0, s1 in ((0, 512), (512, 1024)):
            spread = psum.tile([P, 512], F32, name="spread", tag=f"dx{1 - s0 // 512}")
            for c in range(s0, s1, P):
                nc.tensor.transpose(
                    spread[:, c - s0 : c - s0 + P], gate_cols[:, c // P : c // P + 1].to_broadcast([P, P]), identity[:]
                )
            nc.scalar.copy(gates[:, s0:s1], spread[:, 0 : s1 - s0])

        g4 = held.tile([P, PACK, S], F32, name="g4")
        gb = held.tile([P, PACK * S], BF16, name="gb", align_bytes=64)
        g_codes = held.tile([P, S], U32, name="g_codes", align_bytes=64)
        g_scales = held.tile([P, S], U8, name="g_scales", align_bytes=64)
        w2_codes, w2_scales, w1_codes, w1_scales, wb, vb, db = {}, {}, {}, {}, {}, {}, {}
        da_codes, da_scales, dx_banks, dxs = {}, {}, {}, {}

        def gather(j, s0, s1):
            nc.vector.tensor_copy(g4[:, j, s0:s1], dy[j][:].indirect(offsets[:, s0 // 16 : s1 // 16]))

        def gated(s0, s1, eng=nc.vector):
            eng.tensor_tensor(
                gb[:, PACK * s0 : PACK * s1].rearrange("p (c i j) -> p c j i", i=4, j=PACK),
                g4[:, :, s0:s1].rearrange("p j (c i) -> p c j i", i=4),
                gates[:, s0:s1].rearrange("p (c o i) -> p c o i", o=1, i=4).to_broadcast([P, (s1 - s0) // 4, PACK, 4]),
                ALU.mult,
            )

        def quantise_g(s0, s1):
            nc.vector.quantize_mx(
                out=g_codes[:, s0:s1].bitcast(FP8X4), scales=g_scales[:, s0:s1], in_=gb[:, PACK * s0 : PACK * s1]
            )

        def round_w2(e, q, halves=(0, 1), copy=nc.scalar.copy):
            if 0 in halves:
                wb[e, q] = work.tile([P, PACK * PASS], BF16, name="wb", align_bytes=64, bufs=3)
            for h in halves:
                ms = slice(h * 64, (h + 1) * 64)
                copy(
                    out=wb[e, q][:].rearrange("p (t m j) -> p m j t", t=PACK, j=PACK)[:, ms],
                    in_=w2_raw[e, q].rearrange("p j (m t) -> p m j t", t=PACK)[:, ms],
                )

        def round_w2_planes(e, q, t0, copy):
            if t0 == 0:
                wb[e, q] = work.tile([P, PACK * PASS], BF16, name="wb", align_bytes=64, bufs=3)
            copy(
                wb[e, q][:].rearrange("p (t m j) -> p t m j", t=PACK, j=PACK)[:, t0 : t0 + 2],
                w2_raw[e, q].rearrange("p j (m t) -> p t m j", t=PACK)[:, t0 : t0 + 2],
            )

        def on_gpsimd(rounded, values):
            nc.gpsimd.tensor_scalar(rounded, values, 1.0, 0.0, ALU.mult, ALU.add)

        def on_scalar(rounded, values):
            nc.scalar.copy(rounded.rearrange("p t m j -> p m j t"), values.rearrange("p t m j -> p m j t"))

        def quantise_w2(e, q):
            w2_codes[e, q] = work.tile([P, PASS], U32, name="w2_codes", align_bytes=64, bufs=4)
            w2_scales[e, q] = work.tile([P, PASS], U8, name="w2_scales", align_bytes=64, bufs=4)
            nc.vector.quantize_mx(out=w2_codes[e, q][:].bitcast(FP8X4), scales=w2_scales[e, q][:], in_=wb[e, q][:])

        def round_w1(e, passes=(0, 1), k0=0, k1=K):
            if 0 in passes:
                vb[e] = work.tile([P, Q, K * PACK], BF16, name="vb", align_bytes=64)
            for q in passes:
                nc.scalar.copy(
                    out=vb[e][:, q, PACK * k0 : PACK * k1].rearrange("p (c i t) -> p c t i", i=4, t=PACK),
                    in_=w1_raw[e][:, q, :, k0:k1].rearrange("p t (c i) -> p c t i", i=4),
                )

        def quantise_w1(e, c0=0, c1=Q * K):
            if c0 == 0:
                w1_codes[e] = work.tile([P, Q, K], U32, name="w1_codes", align_bytes=64)
                w1_scales[e] = work.tile([P, Q, K], U8, name="w1_scales", align_bytes=64)
            nc.vector.quantize_mx(
                out=w1_codes[e][:].rearrange("p q k -> p (q k)")[:, c0:c1].bitcast(FP8X4),
                scales=w1_scales[e][:].rearrange("p q k -> p (q k)")[:, c0:c1],
                in_=vb[e][:].rearrange("p q k -> p (q k)")[:, PACK * c0 : PACK * c1],
            )

        def hidden(e, q, room=None):
            if room is None:
                own = work.tile([P, C, PACK], BF16, name="db", align_bytes=64, bufs=4)
                room = own[:]
            db[e, q] = room
            for h in range(C // HALF):
                dh = psum.tile([P, PACK, HALF], F32, name="dh", bufs=6)
                s0 = e * C + h * HALF
                for t in range(PACK):
                    wc = slice(t * P, (t + 1) * P)
                    nc.tensor.matmul_mx(
                        out=dh[:, t, :],
                        lhsT=w2_codes[e, q][:, wc].bitcast(FP8X4),
                        lhsT_scale=w2_scales[e, q][:, wc],
                        rhs=g_codes[:, s0 : s0 + HALF].bitcast(FP8X4),
                        rhs_scale=g_scales[:, s0 : s0 + HALF],
                        start=True,
                        stop=True,
                    )
                nc.vector.scalar_tensor_tensor(
                    out=db[e, q][:, h * HALF : (h + 1) * HALF, :],
                    in0=a_raw[e, q][:, :, h * HALF : (h + 1) * HALF].rearrange("p t s -> p s t"),
                    scalar=0.0,
                    in1=dh[:].rearrange("p t s -> p s t"),
                    op0=ALU.max,
                    op1=ALU.mult,
                )

        def quantise_da(e, q):
            if q == 0:
                da_codes[e] = work.tile([P, Q, C], U32, name="da_codes", align_bytes=64)
                da_scales[e] = work.tile([P, Q, C], U8, name="da_scales", align_bytes=64)
            nc.vector.quantize_mx(
                out=da_codes[e][:, q, :].bitcast(FP8X4),
                scales=da_scales[e][:, q, :],
                in_=db[e, q].rearrange("p s t -> p (s t)"),
            )

        def hidden_both(e):
            both = work.tile([P, Q * C, PACK], BF16, name="dboth", align_bytes=64, bufs=1)
            for q in range(Q):
                hidden(e, q, both[:, q * C : (q + 1) * C, :])
            da_codes[e] = work.tile([P, Q, C], U32, name="da_codes", align_bytes=64)
            da_scales[e] = work.tile([P, Q, C], U8, name="da_scales", align_bytes=64)
            nc.vector.quantize_mx(
                out=da_codes[e][:].rearrange("p q s -> p (q s)").bitcast(FP8X4),
                scales=da_scales[e][:].rearrange("p q s -> p (q s)"),
                in_=both[:].rearrange("p s t -> p (s t)"),
            )

        def back(e, r):
            dx_banks[e, r] = psum.tile([P, C], F32, name="dx", tag=f"dx{r}")
            for q in range(Q):
                nc.tensor.matmul_mx(
                    out=dx_banks[e, r][:],
                    lhsT=w1_codes[e][:, q, r * P : (r + 1) * P].bitcast(FP8X4),
                    lhsT_scale=w1_scales[e][:, q, r * P : (r + 1) * P],
                    rhs=da_codes[e][:, q, :].bitcast(FP8X4),
                    rhs_scale=da_scales[e][:, q, :],
                    start=(q == 0),
                    stop=(q == Q - 1),
                )

        def leave(e, r, room=None):
            if room is None:
                own = work.tile([P, C], F32, name="dxs", bufs=4)
                room = own[:]
            dxs[e, r] = room
            nc.scalar.activation(room, dx_banks[e, r][:], COPY, scale=2.0)

        def scatter(e, r):
            nc.vector.tensor_copy(windows[r][:].indirect(offsets[:, e * 16 : (e + 1) * 16]), dxs[e, r])

        def scatter_on_scalar(e, r):
            nc.scalar.activation(windows[r][:].indirect(offsets[:, e * 16 : (e + 1) * 16]), dxs[e, r], COPY)

        for j in range(PACK - 1):
            gather(j, 0, S)
        gather(3, 0, 2 * C)
        gated(0, C)
        quantise_g(0, C)
        gated(C, 2 * C)
        quantise_g(C, 2 * C)
        gather(3, 2 * C, S)
        for e in (0, 1):
            for q in range(Q):
                for h in (0, 1):
                    round_w2(e, q, (h,), nc.vector.tensor_copy if (e, q, h) == (1, 0, 0) else nc.scalar.copy)
                quantise_w2(e, q)
        gated(2 * C, 3 * C)
        quantise_g(2 * C, 3 * C)
        gated(3 * C, S)
        quantise_g(3 * C, S)
        hidden(0, 0)
        hidden(1, 0)
        quantise_da(0, 0)
        quantise_da(1, 0)
        round_w1(0, (0,))
        quantise_w1(0, 0, K)
        hidden(0, 1)
        round_w1(0, (1,))
        quantise_w1(0, K, 2 * K)
        quantise_da(0, 1)
        back(0, 0)
        back(0, 1)
        hidden(1, 1)
        round_w1(1, (0,))
        quantise_w1(1, 0, K)
        quantise_da(1, 1)
        round_w1(1, (1,))
        quantise_w1(1, K, 2 * K)
        leave(0, 0)
        scatter(0, 0)
        leave(0, 1)
        scatter(0, 1)
        back(1, 0)
        back(1, 1)
        leave(1, 0)
        scatter(1, 0)
        round_w2(2, 0)
        quantise_w2(2, 0)
        leave(1, 1, w2_raw[2, 0][:, 3, 0:C])
        scatter(1, 1)
        round_w2_planes(2, 1, 0, on_gpsimd)
        round_w2_planes(2, 1, 2, on_scalar)
        quantise_w2(2, 1)
        hidden(2, 0)
        round_w2(3, 0)
        quantise_w2(3, 0)
        hidden(2, 1)
        quantise_da(2, 0)
        quantise_da(2, 1)
        round_w2(3, 1)
        quantise_w2(3, 1)
        round_w1(2)
        quantise_w1(2)
        back(2, 0)
        back(2, 1)
        hidden(3, 0)
        hidden(3, 1)
        quantise_da(3, 0)
        quantise_da(3, 1)
        round_w1(3, (0,))
        quantise_w1(3, 0, K)
        for r in range(R):
            round_w1(3, (1,), r * P, (r + 1) * P)
            quantise_w1(3, K + r * P, K + (r + 1) * P)
            leave(2, r, w1_raw[3][:, 0, r, :])
            back(3, r)
        leave(3, 0)
        scatter(2, 0)
        scatter(3, 0)
        scatter_on_scalar(2, 1)
        leave(3, 1)
        scatter_on_scalar(3, 1)

        for r in range(R):
            nc.sync.dma_start(out[r * P : (r + 1) * P, :], windows[r][:])
